import numpy as np
import ml_dtypes

BF16 = ml_dtypes.bfloat16


def bf(x):
    return np.asarray(x, np.float32).astype(BF16)


def f32(x):
    return np.asarray(x, np.float32)


def f64(x):
    return np.asarray(x).astype(np.float64)


def striped(idx):
    return np.tile(idx.reshape(-1, 16).T, (8, 1))


S, K, M, N, E, Q = 256, 128, 256, 128, 2, 64


def setup_inputs():
    return {"base": bf(np.random.standard_normal((M, S))), "x": bf(np.random.standard_normal((K, N))), "w": bf(np.random.standard_normal((E, K, M)) / np.sqrt(K)), "c": f32(0.2 + 0.8 * np.random.random_sample((1, S))), "offs": striped(np.random.permutation(S)[:N])}


def reference(base, x, w, c, offs):
    idx = offs[:16].T.reshape(-1)
    z = f64(base).copy()
    for e in range(E):
        z[:, idx[e * Q : (e + 1) * Q]] += f64(w)[e].T @ f64(x)[:, e * Q : (e + 1) * Q]
    return z * f64(c)

@@ -1,0 +1,56 @@
+import concourse.mybir as mybir
+from concourse.masks import make_identity
+
+BF16, F32, U16 = mybir.dt.bfloat16, mybir.dt.float32, mybir.dt.uint16
+
+P = 128
+TOKENS = 256
+FEATURES = 256
+BLOCKS = FEATURES // P
+EXPERTS = 2
+PIECE = 64
+ENTRIES = EXPERTS * PIECE
+PIECE_COLS = PIECE // 16
+
+FLOPS = 2 * P * FEATURES * ENTRIES
+
+
+def tile_scatter_matmul_kernel(tc, base, x, w, c, offs, out):
+    nc = tc.nc
+    with (
+        tc.tile_pool(name="held", bufs=1) as held,
+        tc.psum_pool(name="windows", bufs=1) as windows,
+    ):
+        offsets = held.tile([P, ENTRIES // 16], U16, name="offsets")
+        nc.sync.dma_start(offsets[:], offs)
+
+        ident = held.tile([P, P], BF16, name="ident")
+        make_identity(nc, ident[:])
+
+        base_sb = held.tile([P, BLOCKS, TOKENS], BF16, name="base_sb")
+        nc.scalar.dma_start(base_sb[:], base.rearrange("(b p) t -> p b t", p=P))
+
+        x_sb = held.tile([P, ENTRIES], BF16, name="x_sb")
+        nc.sync.dma_start(x_sb[:], x)
+        w_sb = held.tile([P, EXPERTS, FEATURES], BF16, name="w_sb")
+        nc.sync.dma_start(w_sb[:], w.rearrange("e k m -> k e m"))
+
+        c_sb = held.tile([P, TOKENS], F32, name="c_sb")
+        nc.scalar.dma_start(c_sb[:], c.rearrange("o t -> (o t)").partition_broadcast(P))
+
+        window = [windows.tile([P, TOKENS], F32, name=f"window{b}") for b in range(BLOCKS)]
+        for b in range(BLOCKS):
+            nc.tensor.matmul(window[b][:], ident[:], base_sb[:, b, :], start=True, stop=False)
+
+        for b in range(BLOCKS):
+            for e in range(EXPERTS):
+                nc.tensor.matmul(
+                    window[b][:].indirect(offsets[:, e * PIECE_COLS : (e + 1) * PIECE_COLS]),
+                    w_sb[:, e, b * P : (b + 1) * P],
+                    x_sb[:, e * PIECE : (e + 1) * PIECE],
+                    start=False,
+                    stop=(e == EXPERTS - 1),
+                )
+            result = held.tile([P, TOKENS], F32, name=f"result{b}")
+            nc.vector.tensor_tensor(result[:], window[b][:], c_sb[:], mybir.AluOpType.mult)
+            nc.sync.dma_start(out[b * P : (b + 1) * P, :], result[:])

@@ -27,8 +27,9 @@ def tile_scatter_matmul_kernel(tc, base, x, w, c, offs, out):
         ident = held.tile([P, P], BF16, name="ident")
         make_identity(nc, ident[:])
 
-        base_sb = held.tile([P, BLOCKS, TOKENS], BF16, name="base_sb")
-        nc.scalar.dma_start(base_sb[:], base.rearrange("(b p) t -> p b t", p=P))
+        base_sb = [held.tile([P, TOKENS], BF16, name=f"base_sb{b}") for b in range(BLOCKS)]
+        for b in range(BLOCKS):
+            nc.scalar.dma_start(base_sb[b][:], base[b * P : (b + 1) * P, :])
 
         x_sb = held.tile([P, ENTRIES], BF16, name="x_sb")
         nc.sync.dma_start(x_sb[:], x)
@@ -36,11 +37,11 @@ def tile_scatter_matmul_kernel(tc, base, x, w, c, offs, out):
         nc.sync.dma_start(w_sb[:], w.rearrange("e k m -> k e m"))
 
         c_sb = held.tile([P, TOKENS], F32, name="c_sb")
-        nc.scalar.dma_start(c_sb[:], c.rearrange("o t -> (o t)").partition_broadcast(P))
+        nc.sync.dma_start(c_sb[:], c.rearrange("o t -> (o t)").partition_broadcast(P))
 
         window = [windows.tile([P, TOKENS], F32, name=f"window{b}") for b in range(BLOCKS)]
         for b in range(BLOCKS):
-            nc.tensor.matmul(window[b][:], ident[:], base_sb[:, b, :], start=True, stop=False)
+            nc.tensor.matmul(window[b][:], ident[:], base_sb[b][:], start=True, stop=False)
 
         for b in range(BLOCKS):
             for e in range(EXPERTS):
@@ -53,4 +54,5 @@ def tile_scatter_matmul_kernel(tc, base, x, w, c, offs, out):
                 )
             result = held.tile([P, TOKENS], F32, name=f"result{b}")
             nc.vector.tensor_tensor(result[:], window[b][:], c_sb[:], mybir.AluOpType.mult)
-            nc.sync.dma_start(out[b * P : (b + 1) * P, :], result[:])
+            store_queue = nc.sync if b % 2 == 0 else nc.scalar
+            store_queue.dma_start(out[b * P : (b + 1) * P, :], result[:])

@@ -11,6 +11,8 @@ EXPERTS = 2
 PIECE = 64
 ENTRIES = EXPERTS * PIECE
 PIECE_COLS = PIECE // 16
+BANK_COLS = 512
+WARM_MATMULS = 2
 
 FLOPS = 2 * P * FEATURES * ENTRIES
 
@@ -26,6 +28,12 @@ def tile_scatter_matmul_kernel(tc, base, x, w, c, offs, out):
 
         ident = held.tile([P, P], BF16, name="ident")
         make_identity(nc, ident[:])
+
+        zeros = held.tile([P, BANK_COLS], BF16, name="zeros")
+        nc.vector.memset(zeros[:], 0.0)
+        scratch = windows.tile([P, BANK_COLS], F32, name="scratch")
+        for i in range(WARM_MATMULS):
+            nc.tensor.matmul(scratch[:], zeros[:, 0:P], zeros[:], start=True, stop=True)
 
         base_sb = [held.tile([P, TOKENS], BF16, name=f"base_sb{b}") for b in range(BLOCKS)]
         for b in range(BLOCKS):

@@ -11,8 +11,6 @@ EXPERTS = 2
 PIECE = 64
 ENTRIES = EXPERTS * PIECE
 PIECE_COLS = PIECE // 16
-BANK_COLS = 512
-WARM_MATMULS = 2
 
 FLOPS = 2 * P * FEATURES * ENTRIES
 
@@ -23,17 +21,14 @@ def tile_scatter_matmul_kernel(tc, base, x, w, c, offs, out):
         tc.tile_pool(name="held", bufs=1) as held,
         tc.psum_pool(name="windows", bufs=1) as windows,
     ):
+        c_row = held.tile([1, TOKENS], F32, name="c_row")
+        nc.sync.dma_start(c_row[:], c)
+
         offsets = held.tile([P, ENTRIES // 16], U16, name="offsets")
         nc.sync.dma_start(offsets[:], offs)
 
         ident = held.tile([P, P], BF16, name="ident")
         make_identity(nc, ident[:])
-
-        zeros = held.tile([P, BANK_COLS], BF16, name="zeros")
-        nc.vector.memset(zeros[:], 0.0)
-        scratch = windows.tile([P, BANK_COLS], F32, name="scratch")
-        for i in range(WARM_MATMULS):
-            nc.tensor.matmul(scratch[:], zeros[:, 0:P], zeros[:], start=True, stop=True)
 
         base_sb = [held.tile([P, TOKENS], BF16, name=f"base_sb{b}") for b in range(BLOCKS)]
         for b in range(BLOCKS):
@@ -44,8 +39,12 @@ def tile_scatter_matmul_kernel(tc, base, x, w, c, offs, out):
         w_sb = held.tile([P, EXPERTS, FEATURES], BF16, name="w_sb")
         nc.sync.dma_start(w_sb[:], w.rearrange("e k m -> k e m"))
 
+        ones = held.tile([1, P], F32, name="ones")
+        nc.vector.memset(ones[:], 1.0)
+        c_bank = windows.tile([P, TOKENS], F32, name="c_bank")
+        nc.tensor.matmul(c_bank[:], ones[:], c_row[:], start=True, stop=True)
         c_sb = held.tile([P, TOKENS], F32, name="c_sb")
-        nc.sync.dma_start(c_sb[:], c.rearrange("o t -> (o t)").partition_broadcast(P))
+        nc.vector.tensor_copy(c_sb[:], c_bank[:])
 
         window = [windows.tile([P, TOKENS], F32, name=f"window{b}") for b in range(BLOCKS)]
         for b in range(BLOCKS):

@@ -11,6 +11,7 @@ EXPERTS = 2
 PIECE = 64
 ENTRIES = EXPERTS * PIECE
 PIECE_COLS = PIECE // 16
+SQUARE = 32
 
 FLOPS = 2 * P * FEATURES * ENTRIES
 
@@ -21,30 +22,35 @@ def tile_scatter_matmul_kernel(tc, base, x, w, c, offs, out):
         tc.tile_pool(name="held", bufs=1) as held,
         tc.psum_pool(name="windows", bufs=1) as windows,
     ):
-        c_row = held.tile([1, TOKENS], F32, name="c_row")
-        nc.sync.dma_start(c_row[:], c)
-
-        offsets = held.tile([P, ENTRIES // 16], U16, name="offsets")
-        nc.sync.dma_start(offsets[:], offs)
+        c_rows = held.tile([P, TOKENS], F32, name="c_rows", align_bytes=64)
+        nc.gpsimd.memset(c_rows[:], 0.0)
+        nc.scalar.dma_start(
+            c_rows[0:P:SQUARE, :], c.rearrange("o t -> (o t)").partition_broadcast(P // SQUARE)
+        )
 
         ident = held.tile([P, P], BF16, name="ident")
         make_identity(nc, ident[:])
 
         base_sb = [held.tile([P, TOKENS], BF16, name=f"base_sb{b}") for b in range(BLOCKS)]
         for b in range(BLOCKS):
-            nc.scalar.dma_start(base_sb[b][:], base[b * P : (b + 1) * P, :])
+            nc.sync.dma_start(base_sb[b][:], base[b * P : (b + 1) * P, :])
+
+        offsets = held.tile([P, ENTRIES // 16], U16, name="offsets")
+        nc.sync.dma_start(offsets[:], offs)
 
         x_sb = held.tile([P, ENTRIES], BF16, name="x_sb")
         nc.sync.dma_start(x_sb[:], x)
         w_sb = held.tile([P, EXPERTS, FEATURES], BF16, name="w_sb")
         nc.sync.dma_start(w_sb[:], w.rearrange("e k m -> k e m"))
 
-        ones = held.tile([1, P], F32, name="ones")
-        nc.vector.memset(ones[:], 1.0)
-        c_bank = windows.tile([P, TOKENS], F32, name="c_bank")
-        nc.tensor.matmul(c_bank[:], ones[:], c_row[:], start=True, stop=True)
-        c_sb = held.tile([P, TOKENS], F32, name="c_sb")
-        nc.vector.tensor_copy(c_sb[:], c_bank[:])
+        c_upright = held.tile([P, TOKENS // SQUARE, SQUARE], F32, name="c_upright", align_bytes=64)
+        nc.vector.transpose(c_upright[:].rearrange("p s j -> p (s j)"), c_rows[:])
+        c_repeated = held.tile([P, TOKENS // SQUARE, SQUARE], F32, name="c_repeated", align_bytes=64)
+        nc.vector.tensor_copy(
+            c_repeated[:], c_upright[:, :, 0:1].to_broadcast([P, TOKENS // SQUARE, SQUARE])
+        )
+        c_sb = held.tile([P, TOKENS], F32, name="c_sb", align_bytes=64)
+        nc.vector.transpose(c_sb[:], c_repeated[:].rearrange("p s j -> p (s j)"))
 
         window = [windows.tile([P, TOKENS], F32, name=f"window{b}") for b in range(BLOCKS)]
         for b in range(BLOCKS):

@@ -12,6 +12,7 @@ PIECE = 64
 ENTRIES = EXPERTS * PIECE
 PIECE_COLS = PIECE // 16
 SQUARE = 32
+SQUARES = TOKENS // SQUARE
 
 FLOPS = 2 * P * FEATURES * ENTRIES
 
@@ -22,11 +23,15 @@ def tile_scatter_matmul_kernel(tc, base, x, w, c, offs, out):
         tc.tile_pool(name="held", bufs=1) as held,
         tc.psum_pool(name="windows", bufs=1) as windows,
     ):
-        c_rows = held.tile([P, TOKENS], F32, name="c_rows", align_bytes=64)
-        nc.gpsimd.memset(c_rows[:], 0.0)
+        c_rows = held.tile([SQUARES, P // SQUARE, SQUARE], F32, name="c_rows")
         nc.scalar.dma_start(
-            c_rows[0:P:SQUARE, :], c.rearrange("o t -> (o t)").partition_broadcast(P // SQUARE)
+            c_rows[:],
+            c.rearrange("o (s i) -> (o s) i", i=SQUARE)
+            .unsqueeze(1)
+            .to_broadcast([SQUARES, P // SQUARE, SQUARE]),
         )
+        small_ident = held.tile([SQUARES, SQUARES], F32, name="small_ident")
+        make_identity(nc, small_ident[:])
 
         ident = held.tile([P, P], BF16, name="ident")
         make_identity(nc, ident[:])
@@ -43,11 +48,13 @@ def tile_scatter_matmul_kernel(tc, base, x, w, c, offs, out):
         w_sb = held.tile([P, EXPERTS, FEATURES], BF16, name="w_sb")
         nc.sync.dma_start(w_sb[:], w.rearrange("e k m -> k e m"))
 
-        c_upright = held.tile([P, TOKENS // SQUARE, SQUARE], F32, name="c_upright", align_bytes=64)
-        nc.vector.transpose(c_upright[:].rearrange("p s j -> p (s j)"), c_rows[:])
-        c_repeated = held.tile([P, TOKENS // SQUARE, SQUARE], F32, name="c_repeated", align_bytes=64)
+        c_upright = windows.tile([P, SQUARES], F32, name="c_upright")
+        nc.tensor.matmul(
+            c_upright[:], c_rows[:].rearrange("s q i -> s (q i)"), small_ident[:], start=True, stop=True
+        )
+        c_repeated = held.tile([P, SQUARES, SQUARE], F32, name="c_repeated", align_bytes=64)
         nc.vector.tensor_copy(
-            c_repeated[:], c_upright[:, :, 0:1].to_broadcast([P, TOKENS // SQUARE, SQUARE])
+            c_repeated[:], c_upright[:].unsqueeze(2).to_broadcast([P, SQUARES, SQUARE])
         )
         c_sb = held.tile([P, TOKENS], F32, name="c_sb", align_bytes=64)
         nc.vector.transpose(c_sb[:], c_repeated[:].rearrange("p s j -> p (s j)"))

@@ -24,7 +24,7 @@ def tile_scatter_matmul_kernel(tc, base, x, w, c, offs, out):
         tc.psum_pool(name="windows", bufs=1) as windows,
     ):
         c_rows = held.tile([SQUARES, P // SQUARE, SQUARE], F32, name="c_rows")
-        nc.scalar.dma_start(
+        nc.sync.dma_start(
             c_rows[:],
             c.rearrange("o (s i) -> (o s) i", i=SQUARE)
             .unsqueeze(1)
@@ -38,7 +38,7 @@ def tile_scatter_matmul_kernel(tc, base, x, w, c, offs, out):
 
         base_sb = [held.tile([P, TOKENS], BF16, name=f"base_sb{b}") for b in range(BLOCKS)]
         for b in range(BLOCKS):
-            nc.sync.dma_start(base_sb[b][:], base[b * P : (b + 1) * P, :])
+            nc.scalar.dma_start(base_sb[b][:], base[b * P : (b + 1) * P, :])
 
         offsets = held.tile([P, ENTRIES // 16], U16, name="offsets")
         nc.sync.dma_start(offsets[:], offs)

@@ -36,9 +36,8 @@ def tile_scatter_matmul_kernel(tc, base, x, w, c, offs, out):
         ident = held.tile([P, P], BF16, name="ident")
         make_identity(nc, ident[:])
 
-        base_sb = [held.tile([P, TOKENS], BF16, name=f"base_sb{b}") for b in range(BLOCKS)]
-        for b in range(BLOCKS):
-            nc.scalar.dma_start(base_sb[b][:], base[b * P : (b + 1) * P, :])
+        base_sb = held.tile([P, BLOCKS, TOKENS], BF16, name="base_sb")
+        nc.scalar.dma_start(base_sb[:], base.rearrange("(b p) t -> p b t", p=P))
 
         offsets = held.tile([P, ENTRIES // 16], U16, name="offsets")
         nc.sync.dma_start(offsets[:], offs)
@@ -61,7 +60,7 @@ def tile_scatter_matmul_kernel(tc, base, x, w, c, offs, out):
 
         window = [windows.tile([P, TOKENS], F32, name=f"window{b}") for b in range(BLOCKS)]
         for b in range(BLOCKS):
-            nc.tensor.matmul(window[b][:], ident[:], base_sb[b][:], start=True, stop=False)
+            nc.tensor.matmul(window[b][:], ident[:], base_sb[:, b, :], start=True, stop=False)
 
         for b in range(BLOCKS):
             for e in range(EXPERTS):
@@ -74,5 +73,5 @@ def tile_scatter_matmul_kernel(tc, base, x, w, c, offs, out):
                 )
             result = held.tile([P, TOKENS], F32, name=f"result{b}")
             nc.vector.tensor_tensor(result[:], window[b][:], c_sb[:], mybir.AluOpType.mult)
-            store_queue = nc.sync if b % 2 == 0 else nc.scalar
+            store_queue = nc.sync if b == BLOCKS - 1 else nc.scalar
             store_queue.dma_start(out[b * P : (b + 1) * P, :], result[:])

@@ -13,6 +13,9 @@ ENTRIES = EXPERTS * PIECE
 PIECE_COLS = PIECE // 16
 SQUARE = 32
 SQUARES = TOKENS // SQUARE
+HALVES = 2
+HALF = TOKENS // HALVES
+HALF_SQUARES = SQUARES // HALVES
 
 FLOPS = 2 * P * FEATURES * ENTRIES
 
@@ -52,11 +55,19 @@ def tile_scatter_matmul_kernel(tc, base, x, w, c, offs, out):
             c_upright[:], c_rows[:].rearrange("s q i -> s (q i)"), small_ident[:], start=True, stop=True
         )
         c_repeated = held.tile([P, SQUARES, SQUARE], F32, name="c_repeated", align_bytes=64)
-        nc.vector.tensor_copy(
-            c_repeated[:], c_upright[:].unsqueeze(2).to_broadcast([P, SQUARES, SQUARE])
-        )
+        for h in range(HALVES):
+            squares = slice(h * HALF_SQUARES, (h + 1) * HALF_SQUARES)
+            nc.vector.tensor_copy(
+                c_repeated[:, squares, :],
+                c_upright[:, squares].unsqueeze(2).to_broadcast([P, HALF_SQUARES, SQUARE]),
+            )
         c_sb = held.tile([P, TOKENS], F32, name="c_sb", align_bytes=64)
-        nc.vector.transpose(c_sb[:], c_repeated[:].rearrange("p s j -> p (s j)"))
+        for h in range(HALVES):
+            squares = slice(h * HALF_SQUARES, (h + 1) * HALF_SQUARES)
+            nc.vector.transpose(
+                c_sb[:, h * HALF : (h + 1) * HALF],
+                c_repeated[:, squares, :].rearrange("p s j -> p (s j)"),
+            )
 
         window = [windows.tile([P, TOKENS], F32, name=f"window{b}") for b in range(BLOCKS)]
         for b in range(BLOCKS):
@@ -72,6 +83,12 @@ def tile_scatter_matmul_kernel(tc, base, x, w, c, offs, out):
                     stop=(e == EXPERTS - 1),
                 )
             result = held.tile([P, TOKENS], F32, name=f"result{b}")
-            nc.vector.tensor_tensor(result[:], window[b][:], c_sb[:], mybir.AluOpType.mult)
+            pieces = HALVES if b == 0 else 1
+            width = TOKENS // pieces
+            for i in range(pieces):
+                columns = slice(i * width, (i + 1) * width)
+                nc.vector.tensor_tensor(
+                    result[:, columns], window[b][:, columns], c_sb[:, columns], mybir.AluOpType.mult
+                )
             store_queue = nc.sync if b == BLOCKS - 1 else nc.scalar
             store_queue.dma_start(out[b * P : (b + 1) * P, :], result[:])

@@ -16,6 +16,8 @@ SQUARES = TOKENS // SQUARE
 HALVES = 2
 HALF = TOKENS // HALVES
 HALF_SQUARES = SQUARES // HALVES
+WARM_UPS = 2
+BANK = 512
 
 FLOPS = 2 * P * FEATURES * ENTRIES
 
@@ -35,6 +37,18 @@ def tile_scatter_matmul_kernel(tc, base, x, w, c, offs, out):
         )
         small_ident = held.tile([SQUARES, SQUARES], F32, name="small_ident")
         make_identity(nc, small_ident[:])
+
+        zeros = held.tile([P, P], BF16, name="zeros")
+        nc.vector.memset(zeros[:], 0.0)
+        unread = windows.tile([P, BANK // P, P], F32, name="unread")
+        for _ in range(WARM_UPS):
+            nc.tensor.matmul(
+                unread[:],
+                zeros[:],
+                zeros[:].unsqueeze(1).to_broadcast([P, BANK // P, P]),
+                start=True,
+                stop=True,
+            )
 
         ident = held.tile([P, P], BF16, name="ident")
         make_identity(nc, ident[:])

@@ -38,14 +38,14 @@ def tile_scatter_matmul_kernel(tc, base, x, w, c, offs, out):
         small_ident = held.tile([SQUARES, SQUARES], F32, name="small_ident")
         make_identity(nc, small_ident[:])
 
-        zeros = held.tile([P, P], BF16, name="zeros")
-        nc.vector.memset(zeros[:], 0.0)
+        ones = held.tile([P, P], BF16, name="ones")
+        nc.vector.memset(ones[:], 1.0)
         unread = windows.tile([P, BANK // P, P], F32, name="unread")
         for _ in range(WARM_UPS):
             nc.tensor.matmul(
                 unread[:],
-                zeros[:],
-                zeros[:].unsqueeze(1).to_broadcast([P, BANK // P, P]),
+                ones[:],
+                ones[:].unsqueeze(1).to_broadcast([P, BANK // P, P]),
                 start=True,
                 stop=True,
             )

import concourse.mybir as mybir
from concourse.masks import make_identity

BF16, F32, U16 = mybir.dt.bfloat16, mybir.dt.float32, mybir.dt.uint16

P = 128
TOKENS = 256
FEATURES = 256
BLOCKS = FEATURES // P
EXPERTS = 2
PIECE = 64
ENTRIES = EXPERTS * PIECE
PIECE_COLS = PIECE // 16
SQUARE = 32
SQUARES = TOKENS // SQUARE
HALVES = 2
HALF = TOKENS // HALVES
HALF_SQUARES = SQUARES // HALVES
WARM_UPS = 2
BANK = 512

FLOPS = 2 * P * FEATURES * ENTRIES


def tile_scatter_matmul_kernel(tc, base, x, w, c, offs, out):
    nc = tc.nc
    with (
        tc.tile_pool(name="held", bufs=1) as held,
        tc.psum_pool(name="windows", bufs=1) as windows,
    ):
        c_rows = held.tile([SQUARES, P // SQUARE, SQUARE], F32, name="c_rows")
        nc.sync.dma_start(
            c_rows[:],
            c.rearrange("o (s i) -> (o s) i", i=SQUARE)
            .unsqueeze(1)
            .to_broadcast([SQUARES, P // SQUARE, SQUARE]),
        )
        small_ident = held.tile([SQUARES, SQUARES], F32, name="small_ident")
        make_identity(nc, small_ident[:])

        ones = held.tile([P, P], BF16, name="ones")
        nc.vector.memset(ones[:], 1.0)
        unread = windows.tile([P, BANK // P, P], F32, name="unread")
        for _ in range(WARM_UPS):
            nc.tensor.matmul(
                unread[:],
                ones[:],
                ones[:].unsqueeze(1).to_broadcast([P, BANK // P, P]),
                start=True,
                stop=True,
            )

        ident = held.tile([P, P], BF16, name="ident")
        make_identity(nc, ident[:])

        base_sb = held.tile([P, BLOCKS, TOKENS], BF16, name="base_sb")
        nc.scalar.dma_start(base_sb[:], base.rearrange("(b p) t -> p b t", p=P))

        offsets = held.tile([P, ENTRIES // 16], U16, name="offsets")
        nc.sync.dma_start(offsets[:], offs)

        x_sb = held.tile([P, ENTRIES], BF16, name="x_sb")
        nc.sync.dma_start(x_sb[:], x)
        w_sb = held.tile([P, EXPERTS, FEATURES], BF16, name="w_sb")
        nc.sync.dma_start(w_sb[:], w.rearrange("e k m -> k e m"))

        c_upright = windows.tile([P, SQUARES], F32, name="c_upright")
        nc.tensor.matmul(
            c_upright[:], c_rows[:].rearrange("s q i -> s (q i)"), small_ident[:], start=True, stop=True
        )
        c_repeated = held.tile([P, SQUARES, SQUARE], F32, name="c_repeated", align_bytes=64)
        for h in range(HALVES):
            squares = slice(h * HALF_SQUARES, (h + 1) * HALF_SQUARES)
            nc.vector.tensor_copy(
                c_repeated[:, squares, :],
                c_upright[:, squares].unsqueeze(2).to_broadcast([P, HALF_SQUARES, SQUARE]),
            )
        c_sb = held.tile([P, TOKENS], F32, name="c_sb", align_bytes=64)
        for h in range(HALVES):
            squares = slice(h * HALF_SQUARES, (h + 1) * HALF_SQUARES)
            nc.vector.transpose(
                c_sb[:, h * HALF : (h + 1) * HALF],
                c_repeated[:, squares, :].rearrange("p s j -> p (s j)"),
            )

        window = [windows.tile([P, TOKENS], F32, name=f"window{b}") for b in range(BLOCKS)]
        for b in range(BLOCKS):
            nc.tensor.matmul(window[b][:], ident[:], base_sb[:, b, :], start=True, stop=False)

        for b in range(BLOCKS):
            for e in range(EXPERTS):
                nc.tensor.matmul(
                    window[b][:].indirect(offsets[:, e * PIECE_COLS : (e + 1) * PIECE_COLS]),
                    w_sb[:, e, b * P : (b + 1) * P],
                    x_sb[:, e * PIECE : (e + 1) * PIECE],
                    start=False,
                    stop=(e == EXPERTS - 1),
                )
            result = held.tile([P, TOKENS], F32, name=f"result{b}")
            pieces = HALVES if b == 0 else 1
            width = TOKENS // pieces
            for i in range(pieces):
                columns = slice(i * width, (i + 1) * width)
                nc.vector.tensor_tensor(
                    result[:, columns], window[b][:, columns], c_sb[:, columns], mybir.AluOpType.mult
                )
            store_queue = nc.sync if b == BLOCKS - 1 else nc.scalar
            store_queue.dma_start(out[b * P : (b + 1) * P, :], result[:])
